import numpy as np
import ml_dtypes


def mxq(x, axis, fmt="e4m3"):
    dtype, down = {"e4m3": (ml_dtypes.float8_e4m3fn, 7), "e5m2": (ml_dtypes.float8_e5m2, 14)}[fmt]
    v = np.moveaxis(np.asarray(x, np.float32).astype(ml_dtypes.bfloat16).astype(np.float64), axis, -1)
    blocks = v.reshape(v.shape[:-1] + (-1, 32))
    amax = np.abs(blocks).max(-1, keepdims=True)
    byte = np.maximum(np.where(amax > 0, np.frexp(amax)[1] - 1 + 127, 0) - down, 1)
    scale = np.exp2(byte - 127.0)
    codes = (blocks / scale).astype(np.float32).astype(dtype).astype(np.float64)
    return np.moveaxis((codes * scale).reshape(v.shape), -1, axis)


WIDE = False


def mx_kscale(k):
    if not WIDE:
        return np.ones(k)
    levels = np.array([30, -30])
    if k % 512:
        return np.exp2(np.random.permutation(np.resize(levels, k // 32))).repeat(32)
    a = np.empty((k // 512, 16))
    for p in range(k // 512):
        a[p, :8] = np.random.permutation(np.resize(levels, 8))
        for g in range(8):
            far = levels[np.abs(levels - a[p, g]) >= 10]
            a[p, g + 8] = far[np.random.randint(len(far))]
    return np.exp2(a.ravel()).repeat(32)


def f64(x):
    return np.asarray(x).astype(np.float64)


def striped(idx):
    return np.tile(np.asarray(idx).reshape(-1, 16).T, (8, 1)).astype(np.uint16)


def unstriped(offs):
    return offs[:16].T.reshape(-1).astype(np.int64)


E2M1 = np.array([0.0, 0.5, 1.0, 1.5, 2.0, 3.0, 4.0, 6.0, -0.0, -0.5, -1.0, -1.5, -2.0, -3.0, -4.0, -6.0])


def pack_weight(w, fmt):
    k, n = w.shape
    w = f64(np.asarray(w, np.float32).astype(ml_dtypes.bfloat16)).reshape(k // 32, 32, n)
    amax = np.abs(w).max(1)
    if fmt in ("e4m3", "e5m2"):
        byte = np.frexp(amax)[1] - 1 + 127 - (7 if fmt == "e4m3" else 14)
    else:
        mant, ex = np.frexp(amax / 6.0)
        byte = np.where(mant > 0.5, ex, ex - 1) + 127
    byte = np.clip(np.where(amax > 0, byte, 1), 1, 254)
    scaled = (w * np.exp2(127.0 - byte)[:, None, :]).reshape(k, n).astype(np.float32)
    by_word = np.ascontiguousarray(scaled.reshape(k // 512, 128, 4, n).transpose(0, 1, 3, 2))
    if fmt in ("e4m3", "e5m2"):
        words = by_word.astype(ml_dtypes.float8_e4m3fn if fmt == "e4m3" else ml_dtypes.float8_e5m2).view(np.uint8)
    else:
        c = by_word.astype(ml_dtypes.float4_e2m1fn).view(np.uint8) & 0xF
        words = (c[..., 0::2] | (c[..., 1::2] << 4)).reshape(k // 512, 128, 2 * n)
    return np.ascontiguousarray(words), np.ascontiguousarray(byte.astype(np.uint8).reshape(k // 512, 16, n))


def unpack_weight(words, scales, fmt):
    g, _, n = scales.shape
    words = np.ascontiguousarray(words).reshape(g, 128, n, -1)
    if fmt in ("e4m3", "e5m2"):
        vals = words.view(ml_dtypes.float8_e4m3fn if fmt == "e4m3" else ml_dtypes.float8_e5m2).astype(np.float64)
    else:
        nib = np.empty((g, 128, n, 4), np.uint8)
        nib[..., 0::2] = words & 0xF
        nib[..., 1::2] = words >> 4
        vals = E2M1[nib]
    vals = vals * np.repeat(np.exp2(scales.astype(np.float64) - 127.0), 8, axis=1)[..., None]
    return vals.transpose(0, 1, 3, 2).reshape(g * 512, n)


def sigmoid(v):
    return 1.0 / (1.0 + np.exp(-v))


K, T, J, R, O, N = 512, 1024, 256, 512, 128, 256


def setup_inputs():
    n = np.random.standard_normal
    idx = np.random.permutation(T)[:J]
    idx2 = np.random.permutation(J)[:O]
    idx3 = np.random.permutation(J)[:O]
    fk = mx_kscale(K)
    fr = mx_kscale(R)
    xtp = pack_weight(n((K, T)) / fk[:, None], "e2m1")
    wp = pack_weight(n((K, R)) * 1 / np.sqrt(K) * fk[:, None], "e4m3")
    w2p = pack_weight(n((K, R)) * 1 / np.sqrt(K) * fk[:, None] * fr, "e5m2")
    wbp = pack_weight(n((R, N)) * 1 / np.sqrt(R) / fr[:, None], "e2m1")
    return {
        "xt_words": xtp[0],
        "xt_scales": xtp[1],
        "w_words": wp[0],
        "w_scales": wp[1],
        "w2_words": w2p[0],
        "w2_scales": w2p[1],
        "sg": (np.random.uniform(0.6, 1.6, (R, 1))).astype(np.float32),
        "wb_words": wbp[0],
        "wb_scales": wbp[1],
        "offs": striped(idx),
        "offs2": striped(idx2),
        "offs3": striped(idx3),
    }


def reference(xt_words, xt_scales, w_words, w_scales, w2_words, w2_scales, sg, wb_words, wb_scales, offs, offs2, offs3):
    idx = unstriped(offs)
    idx2 = unstriped(offs2)
    idx3 = unstriped(offs3)
    xtu = unpack_weight(xt_words, xt_scales, "e2m1")
    wu = unpack_weight(w_words, w_scales, "e4m3")
    w2u = unpack_weight(w2_words, w2_scales, "e5m2")
    wbu = unpack_weight(wb_words, wb_scales, "e2m1")
    xtidxg = xtu[:, idx]
    a = wu.T @ xtidxg
    b = w2u.T @ xtidxg
    hid = np.maximum(b[:, idx2], b[:, idx3]) * sigmoid(a[:, idx3] * f64(sg))
    hidq = mxq(hid, 0, "e5m2")
    y = wbu.T @ hidq
    return y

@@ -1,0 +1,139 @@
+from contextlib import ExitStack
+
+import concourse.mybir as mybir
+
+K, T, J, R, O, N = 512, 1024, 256, 512, 128, 256
+FLOPS = 2 * (2 * K * R * J + R * N * O)
+
+F32 = mybir.dt.float32
+BF16 = mybir.dt.bfloat16
+I32 = mybir.dt.int32
+U32 = mybir.dt.uint32
+U16 = mybir.dt.uint16
+U8 = mybir.dt.uint8
+E4M3 = mybir.dt.float8_e4m3fn_x4
+E5M2 = mybir.dt.float8_e5m2_x4
+E2M1 = mybir.dt.float4_e2m1fn_x4
+ACT = mybir.ActivationFunctionType
+ALU = mybir.AluOpType
+
+P = 128
+PACK = 4
+
+
+def load_scale_rows(queue, plane, scales, q):
+    queue.dma_start(out=plane[32 * q:32 * q + 4, :].bitcast(I32), in_=scales[0, 4 * q:4 * q + 4, :].bitcast(I32))
+
+
+def deal(copy, dst, src, run):
+    copy(out=dst[:].rearrange("p t (c i) -> p c t i", i=run),
+         in_=src[:].rearrange("p (c i t) -> p c t i", i=run, t=PACK))
+
+
+def tile_list_twow_agree_one_plain_kernel(tc, xt_words, xt_scales, w_words, w_scales, w2_words, w2_scales, sg,
+                                              wb_words, wb_scales, offs, offs2, offs3, out):
+    nc = tc.nc
+    with ExitStack() as ctx:
+        sb = ctx.enter_context(tc.tile_pool(name="sb", bufs=1))
+        ps = ctx.enter_context(tc.psum_pool(name="ps", bufs=1))
+
+        idx = sb.tile([P, J // 16], U16, name="idx")
+        idx2 = sb.tile([P, O // 16], U16, name="idx2")
+        idx3 = sb.tile([P, O // 16], U16, name="idx3")
+        x_words = sb.tile([P, T], U16, name="x_words", align_bytes=64)
+        x_plane = sb.tile([P, T], U8, name="x_plane", align_bytes=64)
+        w1_raw = sb.tile([P, R], U32, name="w1_raw", align_bytes=64)
+        w2_raw = sb.tile([P, R], U32, name="w2_raw", align_bytes=64)
+        w1_plane_raw = sb.tile([P, R], U8, name="w1_plane_raw", align_bytes=64)
+        w2_plane_raw = sb.tile([P, R], U8, name="w2_plane_raw", align_bytes=64)
+        wo_words = sb.tile([P, 2 * N], U8, name="wo_words", align_bytes=64)
+        wo_plane = sb.tile([P, N], U8, name="wo_plane", align_bytes=64)
+        slope = sb.tile([P, PACK], F32, name="slope")
+
+        nc.vector.memset(x_plane[:].bitcast(I32), 0)
+        nc.gpsimd.memset(w1_plane_raw[:].bitcast(I32), 0)
+        nc.vector.memset(w2_plane_raw[:].bitcast(I32), 0)
+        nc.vector.memset(wo_plane[:].bitcast(I32), 0)
+
+        nc.sync.dma_start(idx[:], offs)
+        load_scale_rows(nc.scalar, x_plane, xt_scales, 0)
+        load_scale_rows(nc.sync, x_plane, xt_scales, 1)
+        load_scale_rows(nc.scalar, x_plane, xt_scales, 2)
+        nc.sync.dma_start(out=x_words[:].bitcast(I32), in_=xt_words[0].bitcast(I32))
+        load_scale_rows(nc.scalar, x_plane, xt_scales, 3)
+        nc.sync.dma_start(out=w2_raw[:].bitcast(I32), in_=w2_words[0].rearrange("p c t -> p (c t)").bitcast(I32))
+        load_scale_rows(nc.scalar, w2_plane_raw, w2_scales, 0)
+        for q in range(1, 4):
+            load_scale_rows(nc.gpsimd, w1_plane_raw, w_scales, q)
+        for q in range(1, 4):
+            load_scale_rows(nc.sync, w2_plane_raw, w2_scales, q)
+        nc.sync.dma_start(out=w1_raw[:].bitcast(I32), in_=w_words[0].rearrange("p c t -> p (c t)").bitcast(I32))
+        nc.sync.dma_start(idx2[:], offs2)
+        nc.sync.dma_start(idx3[:], offs3)
+        load_scale_rows(nc.sync, w1_plane_raw, w_scales, 0)
+        nc.sync.dma_start(out=slope[:], in_=sg.rearrange("(p t) o -> p (t o)", t=PACK))
+        nc.sync.dma_start(out=wo_words[:].bitcast(I32), in_=wb_words[0].bitcast(I32))
+        for q in range(4):
+            load_scale_rows(nc.sync, wo_plane, wb_scales, q)
+
+
+        xg_words = sb.tile([P, J], U16, name="xg_words", align_bytes=64)
+        xg_plane = sb.tile([P, J], U8, name="xg_plane", align_bytes=64)
+        w1 = sb.tile([P, PACK, P], U32, name="w1", align_bytes=64)
+        w2 = sb.tile([P, PACK, P], U32, name="w2", align_bytes=64)
+        w1_plane = sb.tile([P, PACK, P], U8, name="w1_plane", align_bytes=64)
+        w2_plane = sb.tile([P, PACK, P], U8, name="w2_plane", align_bytes=64)
+
+        nc.vector.tensor_copy(xg_plane[:], x_plane[:].indirect(idx[:]))
+        nc.vector.tensor_copy(xg_words[:], x_words[:].indirect(idx[:]))
+        deal(nc.scalar.copy, w2, w2_raw, 4)
+        deal(nc.vector.tensor_copy, w2_plane, w2_plane_raw, 16)
+        deal(nc.scalar.copy, w1, w1_raw, 4)
+        deal(nc.vector.tensor_copy, w1_plane, w1_plane_raw, 16)
+
+        xg4 = xg_words[:].bitcast(E2M1)
+
+        def product(name, words, plane, fmt, t):
+            acc = ps.tile([P, J], F32, name="acc_%s%d" % (name, t))
+            nc.tensor.matmul_mx(out=acc[:], lhsT=words[:, t, :].bitcast(fmt), lhsT_scale=plane[:, t, :],
+                                rhs=xg4, rhs_scale=xg_plane[:], start=True, stop=True)
+            return acc
+
+        def rows_of(name, t, acc, copy):
+            rows = sb.tile([P, J], F32, name="%s%d" % (name, t))
+            copy(out=rows[:], in_=acc[:])
+            return rows
+
+        g2 = sb.tile([P, PACK, O], F32, name="g2")
+        g3 = sb.tile([P, PACK, O], F32, name="g3")
+        gate = sb.tile([P, PACK, O], F32, name="gate")
+        hid = sb.tile([P, O * PACK], BF16, name="hid", align_bytes=64)
+        hid_walk = hid[:].rearrange("p (c i t) -> p c t i", i=4, t=PACK)
+
+        def walk(tile):
+            return tile[:].rearrange("p t (c i) -> p c t i", i=4)
+
+        top = sb.tile([P, PACK, O], F32, name="top")
+        b_rows = [rows_of("b", t, product("b", w2, w2_plane, E5M2, t), nc.scalar.copy) for t in range(PACK)]
+        a_rows = [rows_of("a", t, product("a", w1, w1_plane, E4M3, t), nc.scalar.copy) for t in range(PACK)]
+        for t in range(PACK):
+            nc.vector.tensor_copy(g2[:, t, :], b_rows[t][:].indirect(idx2[:]))
+            nc.vector.tensor_copy(g3[:, t, :], b_rows[t][:].indirect(idx3[:]))
+        for t in range(PACK):
+            nc.scalar.activation(out=gate[:, t, :], in_=a_rows[t][:].indirect(idx3[:]), func=ACT.Sigmoid,
+                                 scale=slope[:, t:t + 1])
+        nc.vector.tensor_tensor(top[:], g2[:], g3[:], ALU.max)
+        nc.vector.tensor_tensor(hid_walk, walk(top), walk(gate), ALU.mult)
+
+        h_words = sb.tile([P, O], U32, name="h_words", align_bytes=64)
+        h_plane = sb.tile([P, O], U8, name="h_plane", align_bytes=64)
+        nc.vector.quantize_mx(out=h_words[:].bitcast(E5M2), scales=h_plane[:], in_=hid[:])
+
+        for h, (copy, queue) in enumerate(((nc.vector.tensor_copy, nc.sync), (nc.scalar.copy, nc.scalar))):
+            acc = ps.tile([P, O], F32, name="acc_b%d" % h)
+            nc.tensor.matmul_mx(out=acc[:], lhsT=wo_words[:, 2 * P * h:2 * P * (h + 1)].bitcast(E2M1),
+                                lhsT_scale=wo_plane[:, P * h:P * (h + 1)],
+                                rhs=h_words[:].bitcast(E5M2), rhs_scale=h_plane[:], start=True, stop=True)
+            res = sb.tile([P, O], F32, name="res%d" % h)
+            copy(out=res[:], in_=acc[:])
+            queue.dma_start(out=out[P * h:P * (h + 1), :], in_=res[:])

@@ -25,9 +25,8 @@ def load_scale_rows(queue, plane, scales, q):
     queue.dma_start(out=plane[32 * q:32 * q + 4, :].bitcast(I32), in_=scales[0, 4 * q:4 * q + 4, :].bitcast(I32))
 
 
-def deal(copy, dst, src, run):
-    copy(out=dst[:].rearrange("p t (c i) -> p c t i", i=run),
-         in_=src[:].rearrange("p (c i t) -> p c t i", i=run, t=PACK))
+def load_words(queue, tile, words):
+    queue.dma_start(out=tile[:].bitcast(I32), in_=words[0].rearrange("p c t -> p (c t)").bitcast(I32))
 
 
 def tile_list_twow_agree_one_plain_kernel(tc, xt_words, xt_scales, w_words, w_scales, w2_words, w2_scales, sg,
@@ -42,88 +41,100 @@ def tile_list_twow_agree_one_plain_kernel(tc, xt_words, xt_scales, w_words, w_sc
         idx3 = sb.tile([P, O // 16], U16, name="idx3")
         x_words = sb.tile([P, T], U16, name="x_words", align_bytes=64)
         x_plane = sb.tile([P, T], U8, name="x_plane", align_bytes=64)
-        w1_raw = sb.tile([P, R], U32, name="w1_raw", align_bytes=64)
+        w1_raw = sb.tile([P, R], U32, name="w1_raw", tag="w1_raw_then_b", align_bytes=64)
         w2_raw = sb.tile([P, R], U32, name="w2_raw", align_bytes=64)
-        w1_plane_raw = sb.tile([P, R], U8, name="w1_plane_raw", align_bytes=64)
+        w1_plane_raw = sb.tile([P, R], U8, name="w1_plane_raw", tag="w1_plane_then_g2", align_bytes=64)
         w2_plane_raw = sb.tile([P, R], U8, name="w2_plane_raw", align_bytes=64)
         wo_words = sb.tile([P, 2 * N], U8, name="wo_words", align_bytes=64)
         wo_plane = sb.tile([P, N], U8, name="wo_plane", align_bytes=64)
         slope = sb.tile([P, PACK], F32, name="slope")
 
-        nc.vector.memset(x_plane[:].bitcast(I32), 0)
-        nc.gpsimd.memset(w1_plane_raw[:].bitcast(I32), 0)
-        nc.vector.memset(w2_plane_raw[:].bitcast(I32), 0)
-        nc.vector.memset(wo_plane[:].bitcast(I32), 0)
+        for plane in (w2_plane_raw, w1_plane_raw, wo_plane):
+            nc.vector.memset(plane[:].bitcast(I32), 0)
+        warm = sb.tile([P, 2], F32, name="warm")
+        nc.vector.memset(warm[:, 0:1], 0.0)
+        nc.scalar.activation(out=warm[:, 1:2], in_=warm[:, 0:1], func=ACT.Sigmoid)
+
 
         nc.sync.dma_start(idx[:], offs)
-        load_scale_rows(nc.scalar, x_plane, xt_scales, 0)
-        load_scale_rows(nc.sync, x_plane, xt_scales, 1)
-        load_scale_rows(nc.scalar, x_plane, xt_scales, 2)
+        for q, queue in enumerate((nc.scalar, nc.sync, nc.scalar, nc.scalar)):
+            rows = xt_scales[0, 4 * q:4 * q + 4, :].bitcast(I32)
+            queue.dma_start(out=x_plane[32 * q:32 * q + 32, :].bitcast(I32),
+                            in_=rows.unsqueeze(0).broadcast_to([8, 4, T // 4]))
         nc.sync.dma_start(out=x_words[:].bitcast(I32), in_=xt_words[0].bitcast(I32))
-        load_scale_rows(nc.scalar, x_plane, xt_scales, 3)
-        nc.sync.dma_start(out=w2_raw[:].bitcast(I32), in_=w2_words[0].rearrange("p c t -> p (c t)").bitcast(I32))
-        load_scale_rows(nc.scalar, w2_plane_raw, w2_scales, 0)
-        for q in range(1, 4):
-            load_scale_rows(nc.gpsimd, w1_plane_raw, w_scales, q)
-        for q in range(1, 4):
+        load_words(nc.sync, w2_raw, w2_words)
+        for q in range(4):
             load_scale_rows(nc.sync, w2_plane_raw, w2_scales, q)
-        nc.sync.dma_start(out=w1_raw[:].bitcast(I32), in_=w_words[0].rearrange("p c t -> p (c t)").bitcast(I32))
+        load_words(nc.sync, w1_raw, w_words)
+        for q in range(4):
+            load_scale_rows(nc.sync, w1_plane_raw, w_scales, q)
         nc.sync.dma_start(idx2[:], offs2)
         nc.sync.dma_start(idx3[:], offs3)
-        load_scale_rows(nc.sync, w1_plane_raw, w_scales, 0)
         nc.sync.dma_start(out=slope[:], in_=sg.rearrange("(p t) o -> p (t o)", t=PACK))
         nc.sync.dma_start(out=wo_words[:].bitcast(I32), in_=wb_words[0].bitcast(I32))
         for q in range(4):
             load_scale_rows(nc.sync, wo_plane, wb_scales, q)
 
-
         xg_words = sb.tile([P, J], U16, name="xg_words", align_bytes=64)
         xg_plane = sb.tile([P, J], U8, name="xg_plane", align_bytes=64)
-        w1 = sb.tile([P, PACK, P], U32, name="w1", align_bytes=64)
-        w2 = sb.tile([P, PACK, P], U32, name="w2", align_bytes=64)
-        w1_plane = sb.tile([P, PACK, P], U8, name="w1_plane", align_bytes=64)
-        w2_plane = sb.tile([P, PACK, P], U8, name="w2_plane", align_bytes=64)
-
         nc.vector.tensor_copy(xg_plane[:], x_plane[:].indirect(idx[:]))
         nc.vector.tensor_copy(xg_words[:], x_words[:].indirect(idx[:]))
-        deal(nc.scalar.copy, w2, w2_raw, 4)
-        deal(nc.vector.tensor_copy, w2_plane, w2_plane_raw, 16)
-        deal(nc.scalar.copy, w1, w1_raw, 4)
-        deal(nc.vector.tensor_copy, w1_plane, w1_plane_raw, 16)
-
         xg4 = xg_words[:].bitcast(E2M1)
+
+        w1 = sb.tile([P, PACK, P], U32, name="w1", align_bytes=64)
+        w2 = sb.tile([P, PACK, P], U32, name="w2", align_bytes=64)
+
+        def deal_plane(raw, t):
+            plane = sb.tile([P, P], U8, name="plane%d" % t, align_bytes=64)
+            nc.vector.tensor_copy(out=plane[:], in_=raw[:, t::PACK])
+            return plane
 
         def product(name, words, plane, fmt, t):
             acc = ps.tile([P, J], F32, name="acc_%s%d" % (name, t))
-            nc.tensor.matmul_mx(out=acc[:], lhsT=words[:, t, :].bitcast(fmt), lhsT_scale=plane[:, t, :],
+            nc.tensor.matmul_mx(out=acc[:], lhsT=words[:, t, :].bitcast(fmt), lhsT_scale=plane[:],
                                 rhs=xg4, rhs_scale=xg_plane[:], start=True, stop=True)
             return acc
 
-        def rows_of(name, t, acc, copy):
-            rows = sb.tile([P, J], F32, name="%s%d" % (name, t))
-            copy(out=rows[:], in_=acc[:])
-            return rows
+        b_acc = []
+        for t in range(PACK):
+            nc.scalar.copy(out=w2[:, t, :], in_=w2_raw[:, t::PACK])
+            b_acc.append(product("b", w2, deal_plane(w2_plane_raw, t), E5M2, t))
+        nc.scalar.copy(out=w1[:].rearrange("p t (c i) -> p c t i", i=4),
+                       in_=w1_raw[:].rearrange("p (c i t) -> p c t i", i=4, t=PACK))
 
-        g2 = sb.tile([P, PACK, O], F32, name="g2")
+        b_rows, a_rows = [], []
+        for t in range(PACK):
+            tag = "w1_raw_then_b" if t == 2 else "b%d" % t
+            rows = sb.tile([P, J], F32, name="b%d" % t, tag=tag, align_bytes=64)
+            if t < 2:
+                nc.vector.tensor_copy(out=rows[:], in_=b_acc[t][:])
+            else:
+                nc.scalar.copy(out=rows[:], in_=b_acc[t][:])
+            b_rows.append(rows)
+        for t in range(PACK):
+            acc = product("a", w1, deal_plane(w1_plane_raw, t), E4M3, t)
+            rows = sb.tile([P, J], F32, name="a%d" % t)
+            nc.scalar.copy(out=rows[:], in_=acc[:])
+            a_rows.append(rows)
+
+        g2 = sb.tile([P, PACK, O], F32, name="g2", tag="w1_plane_then_g2", align_bytes=64)
         g3 = sb.tile([P, PACK, O], F32, name="g3")
         gate = sb.tile([P, PACK, O], F32, name="gate")
-        hid = sb.tile([P, O * PACK], BF16, name="hid", align_bytes=64)
-        hid_walk = hid[:].rearrange("p (c i t) -> p c t i", i=4, t=PACK)
-
-        def walk(tile):
-            return tile[:].rearrange("p t (c i) -> p c t i", i=4)
-
         top = sb.tile([P, PACK, O], F32, name="top")
-        b_rows = [rows_of("b", t, product("b", w2, w2_plane, E5M2, t), nc.scalar.copy) for t in range(PACK)]
-        a_rows = [rows_of("a", t, product("a", w1, w1_plane, E4M3, t), nc.scalar.copy) for t in range(PACK)]
+        hid = sb.tile([P, O * PACK], BF16, name="hid", align_bytes=64)
         for t in range(PACK):
             nc.vector.tensor_copy(g2[:, t, :], b_rows[t][:].indirect(idx2[:]))
-            nc.vector.tensor_copy(g3[:, t, :], b_rows[t][:].indirect(idx3[:]))
+            if t < PACK - 1:
+                nc.vector.tensor_copy(g3[:, t, :], b_rows[t][:].indirect(idx3[:]))
+            else:
+                nc.scalar.activation(out=g3[:, t, :], in_=b_rows[t][:].indirect(idx3[:]), func=ACT.Copy)
         for t in range(PACK):
             nc.scalar.activation(out=gate[:, t, :], in_=a_rows[t][:].indirect(idx3[:]), func=ACT.Sigmoid,
                                  scale=slope[:, t:t + 1])
         nc.vector.tensor_tensor(top[:], g2[:], g3[:], ALU.max)
-        nc.vector.tensor_tensor(hid_walk, walk(top), walk(gate), ALU.mult)
+        nc.vector.tensor_tensor(hid[:].rearrange("p (c i t) -> p c t i", i=4, t=PACK),
+                                top[:].rearrange("p t (c i) -> p c t i", i=4),
+                                gate[:].rearrange("p t (c i) -> p c t i", i=4), ALU.mult)
 
         h_words = sb.tile([P, O], U32, name="h_words", align_bytes=64)
         h_plane = sb.tile([P, O], U8, name="h_plane", align_bytes=64)

from contextlib import ExitStack

import concourse.mybir as mybir

K, T, J, R, O, N = 512, 1024, 256, 512, 128, 256
FLOPS = 2 * (2 * K * R * J + R * N * O)

F32 = mybir.dt.float32
BF16 = mybir.dt.bfloat16
I32 = mybir.dt.int32
U32 = mybir.dt.uint32
U16 = mybir.dt.uint16
U8 = mybir.dt.uint8
E4M3 = mybir.dt.float8_e4m3fn_x4
E5M2 = mybir.dt.float8_e5m2_x4
E2M1 = mybir.dt.float4_e2m1fn_x4
ACT = mybir.ActivationFunctionType
ALU = mybir.AluOpType

P = 128
PACK = 4


def load_scale_rows(queue, plane, scales, q):
    queue.dma_start(out=plane[32 * q:32 * q + 4, :].bitcast(I32), in_=scales[0, 4 * q:4 * q + 4, :].bitcast(I32))


def load_words(queue, tile, words):
    queue.dma_start(out=tile[:].bitcast(I32), in_=words[0].rearrange("p c t -> p (c t)").bitcast(I32))


def tile_list_twow_agree_one_plain_kernel(tc, xt_words, xt_scales, w_words, w_scales, w2_words, w2_scales, sg,
                                              wb_words, wb_scales, offs, offs2, offs3, out):
    nc = tc.nc
    with ExitStack() as ctx:
        sb = ctx.enter_context(tc.tile_pool(name="sb", bufs=1))
        ps = ctx.enter_context(tc.psum_pool(name="ps", bufs=1))

        idx = sb.tile([P, J // 16], U16, name="idx")
        idx2 = sb.tile([P, O // 16], U16, name="idx2")
        idx3 = sb.tile([P, O // 16], U16, name="idx3")
        x_words = sb.tile([P, T], U16, name="x_words", align_bytes=64)
        x_plane = sb.tile([P, T], U8, name="x_plane", align_bytes=64)
        w1_raw = sb.tile([P, R], U32, name="w1_raw", tag="w1_raw_then_b", align_bytes=64)
        w2_raw = sb.tile([P, R], U32, name="w2_raw", align_bytes=64)
        w1_plane_raw = sb.tile([P, R], U8, name="w1_plane_raw", tag="w1_plane_then_g2", align_bytes=64)
        w2_plane_raw = sb.tile([P, R], U8, name="w2_plane_raw", align_bytes=64)
        wo_words = sb.tile([P, 2 * N], U8, name="wo_words", align_bytes=64)
        wo_plane = sb.tile([P, N], U8, name="wo_plane", align_bytes=64)
        slope = sb.tile([P, PACK], F32, name="slope")

        for plane in (w2_plane_raw, w1_plane_raw, wo_plane):
            nc.vector.memset(plane[:].bitcast(I32), 0)
        warm = sb.tile([P, 2], F32, name="warm")
        nc.vector.memset(warm[:, 0:1], 0.0)
        nc.scalar.activation(out=warm[:, 1:2], in_=warm[:, 0:1], func=ACT.Sigmoid)


        nc.sync.dma_start(idx[:], offs)
        for q, queue in enumerate((nc.scalar, nc.sync, nc.scalar, nc.scalar)):
            rows = xt_scales[0, 4 * q:4 * q + 4, :].bitcast(I32)
            queue.dma_start(out=x_plane[32 * q:32 * q + 32, :].bitcast(I32),
                            in_=rows.unsqueeze(0).broadcast_to([8, 4, T // 4]))
        nc.sync.dma_start(out=x_words[:].bitcast(I32), in_=xt_words[0].bitcast(I32))
        load_words(nc.sync, w2_raw, w2_words)
        for q in range(4):
            load_scale_rows(nc.sync, w2_plane_raw, w2_scales, q)
        load_words(nc.sync, w1_raw, w_words)
        for q in range(4):
            load_scale_rows(nc.sync, w1_plane_raw, w_scales, q)
        nc.sync.dma_start(idx2[:], offs2)
        nc.sync.dma_start(idx3[:], offs3)
        nc.sync.dma_start(out=slope[:], in_=sg.rearrange("(p t) o -> p (t o)", t=PACK))
        nc.sync.dma_start(out=wo_words[:].bitcast(I32), in_=wb_words[0].bitcast(I32))
        for q in range(4):
            load_scale_rows(nc.sync, wo_plane, wb_scales, q)

        xg_words = sb.tile([P, J], U16, name="xg_words", align_bytes=64)
        xg_plane = sb.tile([P, J], U8, name="xg_plane", align_bytes=64)
        nc.vector.tensor_copy(xg_plane[:], x_plane[:].indirect(idx[:]))
        nc.vector.tensor_copy(xg_words[:], x_words[:].indirect(idx[:]))
        xg4 = xg_words[:].bitcast(E2M1)

        w1 = sb.tile([P, PACK, P], U32, name="w1", align_bytes=64)
        w2 = sb.tile([P, PACK, P], U32, name="w2", align_bytes=64)

        def deal_plane(raw, t):
            plane = sb.tile([P, P], U8, name="plane%d" % t, align_bytes=64)
            nc.vector.tensor_copy(out=plane[:], in_=raw[:, t::PACK])
            return plane

        def product(name, words, plane, fmt, t):
            acc = ps.tile([P, J], F32, name="acc_%s%d" % (name, t))
            nc.tensor.matmul_mx(out=acc[:], lhsT=words[:, t, :].bitcast(fmt), lhsT_scale=plane[:],
                                rhs=xg4, rhs_scale=xg_plane[:], start=True, stop=True)
            return acc

        b_acc = []
        for t in range(PACK):
            nc.scalar.copy(out=w2[:, t, :], in_=w2_raw[:, t::PACK])
            b_acc.append(product("b", w2, deal_plane(w2_plane_raw, t), E5M2, t))
        nc.scalar.copy(out=w1[:].rearrange("p t (c i) -> p c t i", i=4),
                       in_=w1_raw[:].rearrange("p (c i t) -> p c t i", i=4, t=PACK))

        b_rows, a_rows = [], []
        for t in range(PACK):
            tag = "w1_raw_then_b" if t == 2 else "b%d" % t
            rows = sb.tile([P, J], F32, name="b%d" % t, tag=tag, align_bytes=64)
            if t < 2:
                nc.vector.tensor_copy(out=rows[:], in_=b_acc[t][:])
            else:
                nc.scalar.copy(out=rows[:], in_=b_acc[t][:])
            b_rows.append(rows)
        for t in range(PACK):
            acc = product("a", w1, deal_plane(w1_plane_raw, t), E4M3, t)
            rows = sb.tile([P, J], F32, name="a%d" % t)
            nc.scalar.copy(out=rows[:], in_=acc[:])
            a_rows.append(rows)

        g2 = sb.tile([P, PACK, O], F32, name="g2", tag="w1_plane_then_g2", align_bytes=64)
        g3 = sb.tile([P, PACK, O], F32, name="g3")
        gate = sb.tile([P, PACK, O], F32, name="gate")
        top = sb.tile([P, PACK, O], F32, name="top")
        hid = sb.tile([P, O * PACK], BF16, name="hid", align_bytes=64)
        for t in range(PACK):
            nc.vector.tensor_copy(g2[:, t, :], b_rows[t][:].indirect(idx2[:]))
            if t < PACK - 1:
                nc.vector.tensor_copy(g3[:, t, :], b_rows[t][:].indirect(idx3[:]))
            else:
                nc.scalar.activation(out=g3[:, t, :], in_=b_rows[t][:].indirect(idx3[:]), func=ACT.Copy)
        for t in range(PACK):
            nc.scalar.activation(out=gate[:, t, :], in_=a_rows[t][:].indirect(idx3[:]), func=ACT.Sigmoid,
                                 scale=slope[:, t:t + 1])
        nc.vector.tensor_tensor(top[:], g2[:], g3[:], ALU.max)
        nc.vector.tensor_tensor(hid[:].rearrange("p (c i t) -> p c t i", i=4, t=PACK),
                                top[:].rearrange("p t (c i) -> p c t i", i=4),
                                gate[:].rearrange("p t (c i) -> p c t i", i=4), ALU.mult)

        h_words = sb.tile([P, O], U32, name="h_words", align_bytes=64)
        h_plane = sb.tile([P, O], U8, name="h_plane", align_bytes=64)
        nc.vector.quantize_mx(out=h_words[:].bitcast(E5M2), scales=h_plane[:], in_=hid[:])

        for h, (copy, queue) in enumerate(((nc.vector.tensor_copy, nc.sync), (nc.scalar.copy, nc.scalar))):
            acc = ps.tile([P, O], F32, name="acc_b%d" % h)
            nc.tensor.matmul_mx(out=acc[:], lhsT=wo_words[:, 2 * P * h:2 * P * (h + 1)].bitcast(E2M1),
                                lhsT_scale=wo_plane[:, P * h:P * (h + 1)],
                                rhs=h_words[:].bitcast(E5M2), rhs_scale=h_plane[:], start=True, stop=True)
            res = sb.tile([P, O], F32, name="res%d" % h)
            copy(out=res[:], in_=acc[:])
            queue.dma_start(out=out[P * h:P * (h + 1), :], in_=res[:])
